import numpy as np
import ml_dtypes


def mxq(x, axis, fmt="e4m3"):
    dtype, down = {"e4m3": (ml_dtypes.float8_e4m3fn, 7), "e5m2": (ml_dtypes.float8_e5m2, 14)}[fmt]
    v = np.moveaxis(np.asarray(x, np.float32).astype(ml_dtypes.bfloat16).astype(np.float64), axis, -1)
    blocks = v.reshape(v.shape[:-1] + (-1, 32))
    amax = np.abs(blocks).max(-1, keepdims=True)
    byte = np.maximum(np.where(amax > 0, np.frexp(amax)[1] - 1 + 127, 0) - down, 1)
    scale = np.exp2(byte - 127.0)
    codes = (blocks / scale).astype(np.float32).astype(dtype).astype(np.float64)
    return np.moveaxis((codes * scale).reshape(v.shape), -1, axis)


WIDE = False


def mx_kscale(k):
    if not WIDE:
        return np.ones(k)
    levels = np.array([10, -10, 5, -5, 0])
    if k % 512:
        return np.exp2(np.random.permutation(np.resize(levels, k // 32))).repeat(32)
    a = np.empty((k // 512, 16))
    for p in range(k // 512):
        a[p, :8] = np.random.permutation(np.resize(levels, 8))
        for g in range(8):
            far = levels[np.abs(levels - a[p, g]) >= 10]
            a[p, g + 8] = far[np.random.randint(len(far))]
    return np.exp2(a.ravel()).repeat(32)


def f64(x):
    return np.asarray(x).astype(np.float64)


def striped(idx):
    return np.tile(np.asarray(idx).reshape(-1, 16).T, (8, 1)).astype(np.uint16)


def unstriped(offs):
    return offs[:16].T.reshape(-1).astype(np.int64)


E2M1 = np.array([0.0, 0.5, 1.0, 1.5, 2.0, 3.0, 4.0, 6.0, -0.0, -0.5, -1.0, -1.5, -2.0, -3.0, -4.0, -6.0])


def pack_weight(w, fmt):
    k, n = w.shape
    w = f64(np.asarray(w, np.float32).astype(ml_dtypes.bfloat16)).reshape(k // 32, 32, n)
    amax = np.abs(w).max(1)
    if fmt == "e4m3":
        byte = np.frexp(amax)[1] - 1 + 127 - 7
    else:
        mant, ex = np.frexp(amax / 6.0)
        byte = np.where(mant > 0.5, ex, ex - 1) + 127
    byte = np.clip(np.where(amax > 0, byte, 1), 1, 254)
    scaled = (w * np.exp2(127.0 - byte)[:, None, :]).reshape(k, n).astype(np.float32)
    by_word = np.ascontiguousarray(scaled.reshape(k // 512, 128, 4, n).transpose(0, 1, 3, 2))
    if fmt == "e4m3":
        words = by_word.astype(ml_dtypes.float8_e4m3fn).view(np.uint8)
    else:
        c = by_word.astype(ml_dtypes.float4_e2m1fn).view(np.uint8) & 0xF
        words = (c[..., 0::2] | (c[..., 1::2] << 4)).reshape(k // 512, 128, 2 * n)
    return np.ascontiguousarray(words), np.ascontiguousarray(byte.astype(np.uint8).reshape(k // 512, 16, n))


def unpack_weight(words, scales, fmt):
    g, _, n = scales.shape
    words = np.ascontiguousarray(words).reshape(g, 128, n, -1)
    if fmt == "e4m3":
        vals = words.view(ml_dtypes.float8_e4m3fn).astype(np.float64)
    else:
        nib = np.empty((g, 128, n, 4), np.uint8)
        nib[..., 0::2] = words & 0xF
        nib[..., 1::2] = words >> 4
        vals = E2M1[nib]
    vals = vals * np.repeat(np.exp2(scales.astype(np.float64) - 127.0), 8, axis=1)[..., None]
    return vals.transpose(0, 1, 3, 2).reshape(g * 512, n)


def softplus(v):
    return np.log(1.0 + np.exp(v))


def sigmoid(v):
    return 1.0 / (1.0 + np.exp(-v))


D, E, T, I, Q, G = 512, 512, 2048, 512, 128, 64


def setup_inputs():
    n = np.random.standard_normal
    idx = np.random.permutation(T)[:I]
    fd = mx_kscale(D)
    fe = mx_kscale(E)
    keysp = pack_weight(n((D, T)) / fd[:, None], "e2m1")
    valsp = pack_weight(n((E, T)) / fe[:, None], "e2m1")
    return {
        "query": (n((D, Q)) * 0.8 / np.sqrt(D) * fd[:, None]).astype(np.float32),
        "query2": (n((D, Q)) * 1.0 / np.sqrt(D) * fd[:, None]).astype(np.float32),
        "keys_words": keysp[0],
        "keys_scales": keysp[1],
        "reserve": (np.random.uniform(2.0, 10.0, (Q, 1))).astype(np.float32),
        "gout": (n((E, Q)) * 1 / np.sqrt(E) * fe[:, None]).astype(np.float32),
        "vals_words": valsp[0],
        "vals_scales": valsp[1],
        "old": (0.5 * n((Q, T))).astype(np.float32),
        "offs": striped(idx),
    }


def reference(query, query2, keys_words, keys_scales, reserve, gout, vals_words, vals_scales, old, offs):
    idx = unstriped(offs)
    keysu = unpack_weight(keys_words, keys_scales, "e2m1")
    valsu = unpack_weight(vals_words, vals_scales, "e2m1")
    queryq = mxq(f64(query), 0, "e4m3")
    keysidxg = keysu[:, idx]
    a = queryq.T @ keysidxg
    query2q = mxq(f64(query2), 0, "e4m3")
    b = query2q.T @ keysidxg
    m1 = b.reshape(Q, G, I // G).mean(axis=2)
    q0 = softplus(m1 * 3.0)
    z = np.sum(q0, axis=1, keepdims=True) + f64(reserve)
    pa = np.exp(a)
    s = pa.reshape(Q, G, I // G).sum(axis=2)
    goutq = mxq(f64(gout), 0, "e4m3")
    valsidxg = valsu[:, idx]
    c0 = goutq.T @ valsidxg
    drr = c0 * pa
    dr = drr.reshape(Q, G, I // G).sum(axis=2)
    dz = np.sum(dr * q0 / s / np.square(z) * (-1.0), axis=1, keepdims=True)
    dq0 = dr / z / s + dz
    dm1 = dq0 * sigmoid(m1 * 3.0) * 3.0
    e1 = dm1 / 8.0
    r1 = np.repeat(e1, I // G, axis=1)
    gs = r1 * 1024.0
    gf = np.zeros((Q, T))
    gf[:, idx] = gs
    y = f64(old) + gf
    return y

@@ -1,0 +1,167 @@
+from contextlib import ExitStack
+
+import concourse.mybir as mybir
+
+D, T, I, Q, G = 512, 2048, 512, 128, 64
+PAGE = I // G
+FLOPS = 3 * 2 * D * I * Q
+
+F32 = mybir.dt.float32
+BF16 = mybir.dt.bfloat16
+I32 = mybir.dt.int32
+U32 = mybir.dt.uint32
+U16 = mybir.dt.uint16
+U8 = mybir.dt.uint8
+FP8X4 = mybir.dt.float8_e4m3fn_x4
+FP4X4 = mybir.dt.float4_e2m1fn_x4
+ACT = mybir.ActivationFunctionType
+ALU = mybir.AluOpType
+AX = mybir.AxisListType
+
+P = 128
+PACK = 4
+OUT_CHUNKS = [256, 512, 512, 512, 256]
+
+
+def tile_attend_bpagequotas_s_kernel(
+    tc, query, query2, keys_words, keys_scales, reserve, gout, vals_words, vals_scales, old, offs, out
+):
+    nc = tc.nc
+    with ExitStack() as ctx:
+        sb = ctx.enter_context(tc.tile_pool(name="sb", bufs=1))
+        ps = ctx.enter_context(tc.psum_pool(name="ps", bufs=1))
+
+        offsets = sb.tile([P, I // 16], U16, name="offsets")
+        k_words = sb.tile([P, T], U16, name="k_words", align_bytes=64)
+        v_words = sb.tile([P, T], U16, name="v_words", align_bytes=64)
+        k_bytes = sb.tile([P, T], U8, name="k_bytes", align_bytes=64)
+        v_bytes = sb.tile([P, T], U8, name="v_bytes", align_bytes=64)
+        q_raw = sb.tile([P, PACK, Q], F32, name="q_raw", align_bytes=64)
+        q2_raw = sb.tile([P, PACK, Q], F32, name="q2_raw", align_bytes=64)
+        g_raw = sb.tile([P, PACK, Q], F32, name="g_raw", align_bytes=64)
+        res = sb.tile([P, 1], F32, name="res")
+        acc = sb.tile([P, T], F32, name="acc", align_bytes=64)
+        placed = sb.tile([P, T], F32, name="placed", align_bytes=64)
+
+        nc.vector.memset(k_bytes[:].bitcast(I32), 0)
+        nc.vector.memset(v_bytes[:].bitcast(I32), 0)
+        nc.vector.memset(placed[:], 0.0)
+
+        def load_scales(tile, scales):
+            for r in range(PACK):
+                nc.sync.dma_start(tile[r:P:32, :].bitcast(I32), scales[0, r:16:PACK, :].bitcast(I32))
+
+        def load_rows(tile, rows):
+            nc.sync.dma_start(tile[:], rows.rearrange("(p j) w -> p j w", j=PACK))
+
+        nc.sync.dma_start(offsets[:], offs)
+        load_scales(k_bytes, keys_scales)
+        nc.sync.dma_start(k_words[:].bitcast(I32), keys_words[0].bitcast(I32))
+        load_rows(q2_raw, query2)
+        load_rows(q_raw, query)
+        load_scales(v_bytes, vals_scales)
+        load_rows(g_raw, gout)
+        nc.sync.dma_start(v_words[:].bitcast(I32), vals_words[0].bitcast(I32))
+        nc.sync.dma_start(res[:], reserve)
+        nc.sync.dma_start(acc[:], old)
+
+        qq_bf = sb.tile([P, 2 * Q, PACK], BF16, name="qq_bf", align_bytes=64)
+        g_bf = sb.tile([P, Q, PACK], BF16, name="g_bf", align_bytes=64)
+        qq_codes = sb.tile([P, 2 * Q], U32, name="qq_codes", align_bytes=64)
+        qq_scale = sb.tile([P, 2 * Q], U8, name="qq_scale", align_bytes=64)
+        g_codes = sb.tile([P, Q], U32, name="g_codes", align_bytes=64)
+        g_scale = sb.tile([P, Q], U8, name="g_scale", align_bytes=64)
+        kg_words = sb.tile([P, I], U16, name="kg_words", align_bytes=64)
+        vg_words = sb.tile([P, I], U16, name="vg_words", align_bytes=64)
+        kg_bytes = sb.tile([P, I], U8, name="kg_bytes", align_bytes=64)
+        vg_bytes = sb.tile([P, I], U8, name="vg_bytes", align_bytes=64)
+
+        def weave(dst, raw):
+            nc.scalar.activation(dst, raw[:].rearrange("p j w -> p w j"), ACT.Copy)
+
+        def gather(dst, window):
+            nc.vector.tensor_copy(dst[:], window[:].indirect(offsets[:]))
+
+        def product(bank, codes, scale, words, scale_bytes):
+            nc.tensor.matmul_mx(
+                out=bank[:], lhsT=codes.bitcast(FP8X4), lhsT_scale=scale,
+                rhs=words[:].bitcast(FP4X4), rhs_scale=scale_bytes[:], start=True, stop=True,
+            )
+
+        def small(name):
+            return sb.tile([P, G], F32, name=name, align_bytes=64)
+
+        def column(name):
+            return sb.tile([P, 1], F32, name=name)
+
+        def by_page(ap):
+            return ap.rearrange("p (g j) -> p g j", j=PAGE)
+
+        def spread(tile):
+            return tile[:].unsqueeze(2).to_broadcast([P, G, PAGE])
+
+        a_ps = ps.tile([P, I], F32, name="a_ps")
+        b_ps = ps.tile([P, I], F32, name="b_ps")
+        c_ps = ps.tile([P, I], F32, name="c_ps")
+
+        weave(qq_bf[:, 0:Q, :], q2_raw)
+        weave(qq_bf[:, Q : 2 * Q, :], q_raw)
+        weave(g_bf[:], g_raw)
+
+        gather(kg_bytes, k_bytes)
+        gather(kg_words, k_words)
+        nc.vector.quantize_mx(qq_codes[:].bitcast(FP8X4), qq_scale[:], qq_bf[:].rearrange("p w j -> p (w j)"))
+        product(b_ps, qq_codes[:, 0:Q], qq_scale[:, 0:Q], kg_words, kg_bytes)
+        product(a_ps, qq_codes[:, Q : 2 * Q], qq_scale[:, Q : 2 * Q], kg_words, kg_bytes)
+        gather(vg_bytes, v_bytes)
+
+        b_sum = small("b_sum")
+        nc.vector.tensor_reduce(b_sum[:], by_page(b_ps[:]), AX.X, ALU.add)
+        nc.vector.quantize_mx(g_codes[:].bitcast(FP8X4), g_scale[:], g_bf[:].rearrange("p w j -> p (w j)"))
+        half = I // 2
+        for h in range(2):
+            cols = slice(h * half, (h + 1) * half)
+            nc.vector.tensor_copy(vg_words[:, cols], v_words[:].indirect(offsets[:, h * half // 16 : (h + 1) * half // 16]))
+            nc.tensor.matmul_mx(
+                out=c_ps[:, cols], lhsT=g_codes[:].bitcast(FP8X4), lhsT_scale=g_scale[:],
+                rhs=vg_words[:, cols].bitcast(FP4X4), rhs_scale=vg_bytes[:, cols], start=True, stop=True,
+            )
+
+        pa = sb.tile([P, I], F32, name="pa", align_bytes=64)
+        nc.scalar.activation(pa[:], a_ps[:], ACT.Exp)
+
+        gate = sb.tile([P, I], F32, name="gate", align_bytes=64)
+        tail = gate[:, 0:G]
+        mag, half_tanh, pos, logp = [small(n) for n in ("mag", "half_tanh", "pos", "logp")]
+        pos_sum, log_sum, z_part, z, rz, dz = [column(n) for n in ("pos_sum", "log_sum", "z_part", "z", "rz", "dz")]
+        nc.scalar.activation(mag[:], b_sum[:], ACT.Abs, scale=3.0 / PAGE)
+        nc.scalar.activation(pos[:], b_sum[:], ACT.Relu, scale=3.0 / PAGE, accum_out=pos_sum[:])
+        nc.scalar.activation(half_tanh[:], b_sum[:], ACT.Tanh, scale=1.5 / PAGE)
+        nc.scalar.activation(tail, mag[:], ACT.Exp, scale=-1.0)
+        nc.scalar.activation(z_part[:], pos_sum[:], ACT.Identity, bias=res[:])
+        nc.scalar.activation(logp[:], tail, ACT.Ln, bias=1.0, accum_out=log_sum[:])
+        nc.scalar.activation(z[:], log_sum[:], ACT.Identity, bias=z_part[:])
+        nc.scalar.activation(by_page(gate[:]), spread(half_tanh), ACT.Copy, bias=192.0, scale=192.0)
+
+        s, rs, q0, pq, dr, w, junk = [small(n) for n in ("s", "rs", "q0", "pq", "dr", "w", "junk")]
+        drr = sb.tile([P, I], F32, name="drr", align_bytes=64)
+        nc.vector.tensor_reduce(s[:], by_page(pa[:]), AX.X, ALU.add)
+        nc.vector.tensor_tensor(drr[:], c_ps[:], pa[:], ALU.mult)
+        nc.vector.reciprocal(rs[:], s[:])
+        nc.vector.reciprocal(rz[:], z[:])
+        nc.vector.tensor_tensor(q0[:], pos[:], logp[:], ALU.add)
+        nc.vector.tensor_reduce(dr[:], by_page(drr[:]), AX.X, ALU.add)
+        nc.vector.scalar_tensor_tensor(pq[:], q0[:], rz[:], rs[:], ALU.mult, ALU.mult)
+        nc.vector.tensor_tensor(w[:], dr[:], rs[:], ALU.mult)
+        nc.vector.scalar_tensor_tensor(junk[:], dr[:], -1.0, pq[:], ALU.mult, ALU.mult, accum_out=dz[:])
+
+        grad = sb.tile([P, I], F32, name="grad", align_bytes=64)
+        nc.vector.tensor_scalar(by_page(grad[:]), spread(w), dz[:], rz[:], ALU.add, ALU.mult)
+        nc.vector.tensor_tensor(placed[:].indirect(offsets[:]), grad[:], gate[:], ALU.mult)
+
+        start = 0
+        for width in OUT_CHUNKS:
+            cols = slice(start, start + width)
+            nc.vector.tensor_tensor(acc[:, cols], acc[:, cols], placed[:, cols], ALU.add)
+            nc.sync.dma_start(out[:, cols], acc[:, cols])
+            start = start + width

@@ -20,7 +20,9 @@ AX = mybir.AxisListType
 
 P = 128
 PACK = 4
-OUT_CHUNKS = [256, 512, 512, 512, 256]
+GAIN = 192.0
+V_PAGES = 40
+OUT_CHUNKS = [128, 384, 512, 512, 256, 256]
 
 
 def tile_attend_bpagequotas_s_kernel(
@@ -47,19 +49,19 @@ def tile_attend_bpagequotas_s_kernel(
         nc.vector.memset(v_bytes[:].bitcast(I32), 0)
         nc.vector.memset(placed[:], 0.0)
 
-        def load_scales(tile, scales):
-            for r in range(PACK):
+        def load_scales(tile, scales, rows):
+            for r in rows:
                 nc.sync.dma_start(tile[r:P:32, :].bitcast(I32), scales[0, r:16:PACK, :].bitcast(I32))
 
         def load_rows(tile, rows):
             nc.sync.dma_start(tile[:], rows.rearrange("(p j) w -> p j w", j=PACK))
 
         nc.sync.dma_start(offsets[:], offs)
-        load_scales(k_bytes, keys_scales)
+        load_scales(k_bytes, keys_scales, range(PACK))
         nc.sync.dma_start(k_words[:].bitcast(I32), keys_words[0].bitcast(I32))
         load_rows(q2_raw, query2)
         load_rows(q_raw, query)
-        load_scales(v_bytes, vals_scales)
+        load_scales(v_bytes, vals_scales, range(PACK))
         load_rows(g_raw, gout)
         nc.sync.dma_start(v_words[:].bitcast(I32), vals_words[0].bitcast(I32))
         nc.sync.dma_start(res[:], reserve)
@@ -118,6 +120,9 @@ def tile_attend_bpagequotas_s_kernel(
         b_sum = small("b_sum")
         nc.vector.tensor_reduce(b_sum[:], by_page(b_ps[:]), AX.X, ALU.add)
         nc.vector.quantize_mx(g_codes[:].bitcast(FP8X4), g_scale[:], g_bf[:].rearrange("p w j -> p (w j)"))
+        pa = sb.tile([P, I], F32, name="pa", align_bytes=64)
+        nc.scalar.activation(pa[:], a_ps[:], ACT.Exp)
+        s = small("s")
         half = I // 2
         for h in range(2):
             cols = slice(h * half, (h + 1) * half)
@@ -126,9 +131,6 @@ def tile_attend_bpagequotas_s_kernel(
                 out=c_ps[:, cols], lhsT=g_codes[:].bitcast(FP8X4), lhsT_scale=g_scale[:],
                 rhs=vg_words[:, cols].bitcast(FP4X4), rhs_scale=vg_bytes[:, cols], start=True, stop=True,
             )
-
-        pa = sb.tile([P, I], F32, name="pa", align_bytes=64)
-        nc.scalar.activation(pa[:], a_ps[:], ACT.Exp)
 
         gate = sb.tile([P, I], F32, name="gate", align_bytes=64)
         tail = gate[:, 0:G]
@@ -141,22 +143,22 @@ def tile_attend_bpagequotas_s_kernel(
         nc.scalar.activation(z_part[:], pos_sum[:], ACT.Identity, bias=res[:])
         nc.scalar.activation(logp[:], tail, ACT.Ln, bias=1.0, accum_out=log_sum[:])
         nc.scalar.activation(z[:], log_sum[:], ACT.Identity, bias=z_part[:])
-        nc.scalar.activation(by_page(gate[:]), spread(half_tanh), ACT.Copy, bias=192.0, scale=192.0)
+        nc.scalar.activation(by_page(gate[:]), spread(half_tanh), ACT.Copy, bias=GAIN, scale=GAIN)
 
-        s, rs, q0, pq, dr, w, junk = [small(n) for n in ("s", "rs", "q0", "pq", "dr", "w", "junk")]
+        rs, q0n, dr, w, junk = [small(n) for n in ("rs", "q0n", "dr", "w", "junk")]
         drr = sb.tile([P, I], F32, name="drr", align_bytes=64)
+        grad = sb.tile([P, I], F32, name="grad", align_bytes=64)
         nc.vector.tensor_reduce(s[:], by_page(pa[:]), AX.X, ALU.add)
         nc.vector.tensor_tensor(drr[:], c_ps[:], pa[:], ALU.mult)
         nc.vector.reciprocal(rs[:], s[:])
-        nc.vector.reciprocal(rz[:], z[:])
-        nc.vector.tensor_tensor(q0[:], pos[:], logp[:], ALU.add)
         nc.vector.tensor_reduce(dr[:], by_page(drr[:]), AX.X, ALU.add)
-        nc.vector.scalar_tensor_tensor(pq[:], q0[:], rz[:], rs[:], ALU.mult, ALU.mult)
-        nc.vector.tensor_tensor(w[:], dr[:], rs[:], ALU.mult)
-        nc.vector.scalar_tensor_tensor(junk[:], dr[:], -1.0, pq[:], ALU.mult, ALU.mult, accum_out=dz[:])
+        nc.vector.reciprocal(rz[:], z[:])
+        nc.vector.scalar_tensor_tensor(q0n[:], pos[:], -1.0, logp[:], ALU.mult, ALU.subtract)
+        nc.vector.scalar_tensor_tensor(w[:], dr[:], rz[:], rs[:], ALU.mult, ALU.mult)
+        nc.vector.scalar_tensor_tensor(junk[:], w[:], rz[:], q0n[:], ALU.mult, ALU.mult, accum_out=dz[:])
 
-        grad = sb.tile([P, I], F32, name="grad", align_bytes=64)
-        nc.vector.tensor_scalar(by_page(grad[:]), spread(w), dz[:], rz[:], ALU.add, ALU.mult)
+        nc.vector.tensor_scalar_add(by_page(grad[:])[:, 0:V_PAGES, :], spread(w)[:, 0:V_PAGES, :], dz[:])
+        nc.scalar.activation(by_page(grad[:])[:, V_PAGES:G, :], spread(w)[:, V_PAGES:G, :], ACT.Identity, bias=dz[:])
         nc.vector.tensor_tensor(placed[:].indirect(offsets[:]), grad[:], gate[:], ALU.mult)
 
         start = 0

@@ -22,7 +22,7 @@ P = 128
 PACK = 4
 GAIN = 192.0
 V_PAGES = 40
-OUT_CHUNKS = [128, 384, 512, 512, 256, 256]
+OUT_CHUNKS = [256, 512, 512, 512, 256]
 
 
 def tile_attend_bpagequotas_s_kernel(
@@ -64,7 +64,7 @@ def tile_attend_bpagequotas_s_kernel(
         load_scales(v_bytes, vals_scales, range(PACK))
         load_rows(g_raw, gout)
         nc.sync.dma_start(v_words[:].bitcast(I32), vals_words[0].bitcast(I32))
-        nc.sync.dma_start(res[:], reserve)
+        nc.gpsimd.dma_start(res[:], reserve)
         nc.sync.dma_start(acc[:], old)
 
         qq_bf = sb.tile([P, 2 * Q, PACK], BF16, name="qq_bf", align_bytes=64)

@@ -21,7 +21,6 @@ AX = mybir.AxisListType
 P = 128
 PACK = 4
 GAIN = 192.0
-V_PAGES = 40
 OUT_CHUNKS = [256, 512, 512, 512, 256]
 
 
@@ -56,9 +55,9 @@ def tile_attend_bpagequotas_s_kernel(
         def load_rows(tile, rows):
             nc.sync.dma_start(tile[:], rows.rearrange("(p j) w -> p j w", j=PACK))
 
+        nc.sync.dma_start(k_words[:].bitcast(I32), keys_words[0].bitcast(I32))
         nc.sync.dma_start(offsets[:], offs)
         load_scales(k_bytes, keys_scales, range(PACK))
-        nc.sync.dma_start(k_words[:].bitcast(I32), keys_words[0].bitcast(I32))
         load_rows(q2_raw, query2)
         load_rows(q_raw, query)
         load_scales(v_bytes, vals_scales, range(PACK))
@@ -79,7 +78,9 @@ def tile_attend_bpagequotas_s_kernel(
         vg_bytes = sb.tile([P, I], U8, name="vg_bytes", align_bytes=64)
 
         def weave(dst, raw):
-            nc.scalar.activation(dst, raw[:].rearrange("p j w -> p w j"), ACT.Copy)
+            nc.scalar.activation(
+                dst.rearrange("p (c i) j -> p c j i", i=PACK), raw[:].rearrange("p j (c i) -> p c j i", i=PACK), ACT.Copy
+            )
 
         def gather(dst, window):
             nc.vector.tensor_copy(dst[:], window[:].indirect(offsets[:]))
@@ -132,33 +133,37 @@ def tile_attend_bpagequotas_s_kernel(
                 rhs=vg_words[:, cols].bitcast(FP4X4), rhs_scale=vg_bytes[:, cols], start=True, stop=True,
             )
 
-        gate = sb.tile([P, I], F32, name="gate", align_bytes=64)
-        tail = gate[:, 0:G]
-        mag, half_tanh, pos, logp = [small(n) for n in ("mag", "half_tanh", "pos", "logp")]
-        pos_sum, log_sum, z_part, z, rz, dz = [column(n) for n in ("pos_sum", "log_sum", "z_part", "z", "rz", "dz")]
+        mag, tail, half_tanh, pos, logp = [small(n) for n in ("mag", "tail", "half_tanh", "pos", "logp")]
+        pos_sum, z_part, z_part_s, z, zz, c, dsum = [
+            column(n) for n in ("pos_sum", "z_part", "z_part_s", "z", "zz", "c", "dsum")
+        ]
+        dr = small("dr")
+        log_sum = dr[:, 0:1]
         nc.scalar.activation(mag[:], b_sum[:], ACT.Abs, scale=3.0 / PAGE)
         nc.scalar.activation(pos[:], b_sum[:], ACT.Relu, scale=3.0 / PAGE, accum_out=pos_sum[:])
         nc.scalar.activation(half_tanh[:], b_sum[:], ACT.Tanh, scale=1.5 / PAGE)
-        nc.scalar.activation(tail, mag[:], ACT.Exp, scale=-1.0)
+        nc.scalar.activation(tail[:], mag[:], ACT.Exp, scale=-1.0)
         nc.scalar.activation(z_part[:], pos_sum[:], ACT.Identity, bias=res[:])
-        nc.scalar.activation(logp[:], tail, ACT.Ln, bias=1.0, accum_out=log_sum[:])
-        nc.scalar.activation(z[:], log_sum[:], ACT.Identity, bias=z_part[:])
-        nc.scalar.activation(by_page(gate[:]), spread(half_tanh), ACT.Copy, bias=GAIN, scale=GAIN)
+        nc.scalar.activation(logp[:], tail[:], ACT.Ln, bias=1.0, accum_out=log_sum)
+        nc.scalar.activation(z_part_s[:], z_part[:], ACT.Copy, scale=GAIN**-0.5)
+        nc.scalar.activation(zz[:], log_sum, ACT.Square, bias=z_part_s[:], scale=GAIN**-0.5)
+        nc.scalar.activation(z[:], log_sum, ACT.Identity, bias=z_part[:])
 
-        rs, q0n, dr, w, junk = [small(n) for n in ("rs", "q0n", "dr", "w", "junk")]
+        rs, q0, u, w, junk = [small(n) for n in ("rs", "q0", "u", "w", "junk")]
         drr = sb.tile([P, I], F32, name="drr", align_bytes=64)
+        gate = sb.tile([P, I], F32, name="gate", align_bytes=64)
         grad = sb.tile([P, I], F32, name="grad", align_bytes=64)
         nc.vector.tensor_reduce(s[:], by_page(pa[:]), AX.X, ALU.add)
         nc.vector.tensor_tensor(drr[:], c_ps[:], pa[:], ALU.mult)
         nc.vector.reciprocal(rs[:], s[:])
+        nc.vector.reciprocal(c[:], zz[:])
+        nc.gpsimd.tensor_tensor(q0[:], pos[:], logp[:], ALU.add)
+        nc.gpsimd.tensor_tensor(u[:], q0[:], rs[:], ALU.mult)
+        nc.scalar.activation(by_page(gate[:]), spread(half_tanh), ACT.Identity, bias=c[:], scale=c[:])
         nc.vector.tensor_reduce(dr[:], by_page(drr[:]), AX.X, ALU.add)
-        nc.vector.reciprocal(rz[:], z[:])
-        nc.vector.scalar_tensor_tensor(q0n[:], pos[:], -1.0, logp[:], ALU.mult, ALU.subtract)
-        nc.vector.scalar_tensor_tensor(w[:], dr[:], rz[:], rs[:], ALU.mult, ALU.mult)
-        nc.vector.scalar_tensor_tensor(junk[:], w[:], rz[:], q0n[:], ALU.mult, ALU.mult, accum_out=dz[:])
-
-        nc.vector.tensor_scalar_add(by_page(grad[:])[:, 0:V_PAGES, :], spread(w)[:, 0:V_PAGES, :], dz[:])
-        nc.scalar.activation(by_page(grad[:])[:, V_PAGES:G, :], spread(w)[:, V_PAGES:G, :], ACT.Identity, bias=dz[:])
+        nc.vector.scalar_tensor_tensor(w[:], dr[:], z[:], rs[:], ALU.mult, ALU.mult)
+        nc.vector.scalar_tensor_tensor(junk[:], dr[:], -1.0, u[:], ALU.mult, ALU.mult, accum_out=dsum[:])
+        nc.vector.tensor_scalar_add(by_page(grad[:]), spread(w), dsum[:])
         nc.vector.tensor_tensor(placed[:].indirect(offsets[:]), grad[:], gate[:], ALU.mult)
 
         start = 0

from contextlib import ExitStack

import concourse.mybir as mybir

D, T, I, Q, G = 512, 2048, 512, 128, 64
PAGE = I // G
FLOPS = 3 * 2 * D * I * Q

F32 = mybir.dt.float32
BF16 = mybir.dt.bfloat16
I32 = mybir.dt.int32
U32 = mybir.dt.uint32
U16 = mybir.dt.uint16
U8 = mybir.dt.uint8
FP8X4 = mybir.dt.float8_e4m3fn_x4
FP4X4 = mybir.dt.float4_e2m1fn_x4
ACT = mybir.ActivationFunctionType
ALU = mybir.AluOpType
AX = mybir.AxisListType

P = 128
PACK = 4
GAIN = 192.0
OUT_CHUNKS = [256, 512, 512, 512, 256]


def tile_attend_bpagequotas_s_kernel(
    tc, query, query2, keys_words, keys_scales, reserve, gout, vals_words, vals_scales, old, offs, out
):
    nc = tc.nc
    with ExitStack() as ctx:
        sb = ctx.enter_context(tc.tile_pool(name="sb", bufs=1))
        ps = ctx.enter_context(tc.psum_pool(name="ps", bufs=1))

        offsets = sb.tile([P, I // 16], U16, name="offsets")
        k_words = sb.tile([P, T], U16, name="k_words", align_bytes=64)
        v_words = sb.tile([P, T], U16, name="v_words", align_bytes=64)
        k_bytes = sb.tile([P, T], U8, name="k_bytes", align_bytes=64)
        v_bytes = sb.tile([P, T], U8, name="v_bytes", align_bytes=64)
        q_raw = sb.tile([P, PACK, Q], F32, name="q_raw", align_bytes=64)
        q2_raw = sb.tile([P, PACK, Q], F32, name="q2_raw", align_bytes=64)
        g_raw = sb.tile([P, PACK, Q], F32, name="g_raw", align_bytes=64)
        res = sb.tile([P, 1], F32, name="res")
        acc = sb.tile([P, T], F32, name="acc", align_bytes=64)
        placed = sb.tile([P, T], F32, name="placed", align_bytes=64)

        nc.vector.memset(k_bytes[:].bitcast(I32), 0)
        nc.vector.memset(v_bytes[:].bitcast(I32), 0)
        nc.vector.memset(placed[:], 0.0)

        def load_scales(tile, scales, rows):
            for r in rows:
                nc.sync.dma_start(tile[r:P:32, :].bitcast(I32), scales[0, r:16:PACK, :].bitcast(I32))

        def load_rows(tile, rows):
            nc.sync.dma_start(tile[:], rows.rearrange("(p j) w -> p j w", j=PACK))

        nc.sync.dma_start(k_words[:].bitcast(I32), keys_words[0].bitcast(I32))
        nc.sync.dma_start(offsets[:], offs)
        load_scales(k_bytes, keys_scales, range(PACK))
        load_rows(q2_raw, query2)
        load_rows(q_raw, query)
        load_scales(v_bytes, vals_scales, range(PACK))
        load_rows(g_raw, gout)
        nc.sync.dma_start(v_words[:].bitcast(I32), vals_words[0].bitcast(I32))
        nc.gpsimd.dma_start(res[:], reserve)
        nc.sync.dma_start(acc[:], old)

        qq_bf = sb.tile([P, 2 * Q, PACK], BF16, name="qq_bf", align_bytes=64)
        g_bf = sb.tile([P, Q, PACK], BF16, name="g_bf", align_bytes=64)
        qq_codes = sb.tile([P, 2 * Q], U32, name="qq_codes", align_bytes=64)
        qq_scale = sb.tile([P, 2 * Q], U8, name="qq_scale", align_bytes=64)
        g_codes = sb.tile([P, Q], U32, name="g_codes", align_bytes=64)
        g_scale = sb.tile([P, Q], U8, name="g_scale", align_bytes=64)
        kg_words = sb.tile([P, I], U16, name="kg_words", align_bytes=64)
        vg_words = sb.tile([P, I], U16, name="vg_words", align_bytes=64)
        kg_bytes = sb.tile([P, I], U8, name="kg_bytes", align_bytes=64)
        vg_bytes = sb.tile([P, I], U8, name="vg_bytes", align_bytes=64)

        def weave(dst, raw):
            nc.scalar.activation(
                dst.rearrange("p (c i) j -> p c j i", i=PACK), raw[:].rearrange("p j (c i) -> p c j i", i=PACK), ACT.Copy
            )

        def gather(dst, window):
            nc.vector.tensor_copy(dst[:], window[:].indirect(offsets[:]))

        def product(bank, codes, scale, words, scale_bytes):
            nc.tensor.matmul_mx(
                out=bank[:], lhsT=codes.bitcast(FP8X4), lhsT_scale=scale,
                rhs=words[:].bitcast(FP4X4), rhs_scale=scale_bytes[:], start=True, stop=True,
            )

        def small(name):
            return sb.tile([P, G], F32, name=name, align_bytes=64)

        def column(name):
            return sb.tile([P, 1], F32, name=name)

        def by_page(ap):
            return ap.rearrange("p (g j) -> p g j", j=PAGE)

        def spread(tile):
            return tile[:].unsqueeze(2).to_broadcast([P, G, PAGE])

        a_ps = ps.tile([P, I], F32, name="a_ps")
        b_ps = ps.tile([P, I], F32, name="b_ps")
        c_ps = ps.tile([P, I], F32, name="c_ps")

        weave(qq_bf[:, 0:Q, :], q2_raw)
        weave(qq_bf[:, Q : 2 * Q, :], q_raw)
        weave(g_bf[:], g_raw)

        gather(kg_bytes, k_bytes)
        gather(kg_words, k_words)
        nc.vector.quantize_mx(qq_codes[:].bitcast(FP8X4), qq_scale[:], qq_bf[:].rearrange("p w j -> p (w j)"))
        product(b_ps, qq_codes[:, 0:Q], qq_scale[:, 0:Q], kg_words, kg_bytes)
        product(a_ps, qq_codes[:, Q : 2 * Q], qq_scale[:, Q : 2 * Q], kg_words, kg_bytes)
        gather(vg_bytes, v_bytes)

        b_sum = small("b_sum")
        nc.vector.tensor_reduce(b_sum[:], by_page(b_ps[:]), AX.X, ALU.add)
        nc.vector.quantize_mx(g_codes[:].bitcast(FP8X4), g_scale[:], g_bf[:].rearrange("p w j -> p (w j)"))
        pa = sb.tile([P, I], F32, name="pa", align_bytes=64)
        nc.scalar.activation(pa[:], a_ps[:], ACT.Exp)
        s = small("s")
        half = I // 2
        for h in range(2):
            cols = slice(h * half, (h + 1) * half)
            nc.vector.tensor_copy(vg_words[:, cols], v_words[:].indirect(offsets[:, h * half // 16 : (h + 1) * half // 16]))
            nc.tensor.matmul_mx(
                out=c_ps[:, cols], lhsT=g_codes[:].bitcast(FP8X4), lhsT_scale=g_scale[:],
                rhs=vg_words[:, cols].bitcast(FP4X4), rhs_scale=vg_bytes[:, cols], start=True, stop=True,
            )

        mag, tail, half_tanh, pos, logp = [small(n) for n in ("mag", "tail", "half_tanh", "pos", "logp")]
        pos_sum, z_part, z_part_s, z, zz, c, dsum = [
            column(n) for n in ("pos_sum", "z_part", "z_part_s", "z", "zz", "c", "dsum")
        ]
        dr = small("dr")
        log_sum = dr[:, 0:1]
        nc.scalar.activation(mag[:], b_sum[:], ACT.Abs, scale=3.0 / PAGE)
        nc.scalar.activation(pos[:], b_sum[:], ACT.Relu, scale=3.0 / PAGE, accum_out=pos_sum[:])
        nc.scalar.activation(half_tanh[:], b_sum[:], ACT.Tanh, scale=1.5 / PAGE)
        nc.scalar.activation(tail[:], mag[:], ACT.Exp, scale=-1.0)
        nc.scalar.activation(z_part[:], pos_sum[:], ACT.Identity, bias=res[:])
        nc.scalar.activation(logp[:], tail[:], ACT.Ln, bias=1.0, accum_out=log_sum)
        nc.scalar.activation(z_part_s[:], z_part[:], ACT.Copy, scale=GAIN**-0.5)
        nc.scalar.activation(zz[:], log_sum, ACT.Square, bias=z_part_s[:], scale=GAIN**-0.5)
        nc.scalar.activation(z[:], log_sum, ACT.Identity, bias=z_part[:])

        rs, q0, u, w, junk = [small(n) for n in ("rs", "q0", "u", "w", "junk")]
        drr = sb.tile([P, I], F32, name="drr", align_bytes=64)
        gate = sb.tile([P, I], F32, name="gate", align_bytes=64)
        grad = sb.tile([P, I], F32, name="grad", align_bytes=64)
        nc.vector.tensor_reduce(s[:], by_page(pa[:]), AX.X, ALU.add)
        nc.vector.tensor_tensor(drr[:], c_ps[:], pa[:], ALU.mult)
        nc.vector.reciprocal(rs[:], s[:])
        nc.vector.reciprocal(c[:], zz[:])
        nc.gpsimd.tensor_tensor(q0[:], pos[:], logp[:], ALU.add)
        nc.gpsimd.tensor_tensor(u[:], q0[:], rs[:], ALU.mult)
        nc.scalar.activation(by_page(gate[:]), spread(half_tanh), ACT.Identity, bias=c[:], scale=c[:])
        nc.vector.tensor_reduce(dr[:], by_page(drr[:]), AX.X, ALU.add)
        nc.vector.scalar_tensor_tensor(w[:], dr[:], z[:], rs[:], ALU.mult, ALU.mult)
        nc.vector.scalar_tensor_tensor(junk[:], dr[:], -1.0, u[:], ALU.mult, ALU.mult, accum_out=dsum[:])
        nc.vector.tensor_scalar_add(by_page(grad[:]), spread(w), dsum[:])
        nc.vector.tensor_tensor(placed[:].indirect(offsets[:]), grad[:], gate[:], ALU.mult)

        start = 0
        for width in OUT_CHUNKS:
            cols = slice(start, start + width)
            nc.vector.tensor_tensor(acc[:, cols], acc[:, cols], placed[:, cols], ALU.add)
            nc.sync.dma_start(out[:, cols], acc[:, cols])
            start = start + width
